import numpy as np
import ml_dtypes


def mxq(x, axis, fmt="e4m3"):
    dtype, down = {"e4m3": (ml_dtypes.float8_e4m3fn, 7), "e5m2": (ml_dtypes.float8_e5m2, 14)}[fmt]
    v = np.moveaxis(np.asarray(x, np.float32).astype(ml_dtypes.bfloat16).astype(np.float64), axis, -1)
    blocks = v.reshape(v.shape[:-1] + (-1, 32))
    amax = np.abs(blocks).max(-1, keepdims=True)
    byte = np.maximum(np.where(amax > 0, np.frexp(amax)[1] - 1 + 127, 0) - down, 1)
    scale = np.exp2(byte - 127.0)
    codes = (blocks / scale).astype(np.float32).astype(dtype).astype(np.float64)
    return np.moveaxis((codes * scale).reshape(v.shape), -1, axis)


WIDE = False


def mx_kscale(k):
    if not WIDE:
        return np.ones(k)
    levels = np.array([10, -10, 5, -5, 0])
    if k % 512:
        return np.exp2(np.random.permutation(np.resize(levels, k // 32))).repeat(32)
    a = np.empty((k // 512, 16))
    for p in range(k // 512):
        a[p, :8] = np.random.permutation(np.resize(levels, 8))
        for g in range(8):
            far = levels[np.abs(levels - a[p, g]) >= 10]
            a[p, g + 8] = far[np.random.randint(len(far))]
    return np.exp2(a.ravel()).repeat(32)


def f64(x):
    return np.asarray(x).astype(np.float64)


def striped8(idx):
    return np.asarray(idx).reshape(8, -1, 16).transpose(0, 2, 1).reshape(128, -1).astype(np.uint16)


def unstriped8(offs):
    return offs.reshape(8, 16, -1).transpose(0, 2, 1).reshape(8, -1).astype(np.int64)


def pick8(x, idx, run):
    r = np.arange(len(x))
    return x[r[:, None], idx[r % (8 * run) // run]]


E2M1 = np.array([0.0, 0.5, 1.0, 1.5, 2.0, 3.0, 4.0, 6.0, -0.0, -0.5, -1.0, -1.5, -2.0, -3.0, -4.0, -6.0])


def pack_weight(w, fmt):
    k, n = w.shape
    w = f64(np.asarray(w, np.float32).astype(ml_dtypes.bfloat16)).reshape(k // 32, 32, n)
    amax = np.abs(w).max(1)
    if fmt == "e4m3":
        byte = np.frexp(amax)[1] - 1 + 127 - 7
    else:
        mant, ex = np.frexp(amax / 6.0)
        byte = np.where(mant > 0.5, ex, ex - 1) + 127
    byte = np.clip(np.where(amax > 0, byte, 1), 1, 254)
    scaled = (w * np.exp2(127.0 - byte)[:, None, :]).reshape(k, n).astype(np.float32)
    by_word = np.ascontiguousarray(scaled.reshape(k // 512, 128, 4, n).transpose(0, 1, 3, 2))
    if fmt == "e4m3":
        words = by_word.astype(ml_dtypes.float8_e4m3fn).view(np.uint8)
    else:
        c = by_word.astype(ml_dtypes.float4_e2m1fn).view(np.uint8) & 0xF
        words = (c[..., 0::2] | (c[..., 1::2] << 4)).reshape(k // 512, 128, 2 * n)
    return np.ascontiguousarray(words), np.ascontiguousarray(byte.astype(np.uint8).reshape(k // 512, 16, n))


def unpack_weight(words, scales, fmt):
    g, _, n = scales.shape
    words = np.ascontiguousarray(words).reshape(g, 128, n, -1)
    if fmt == "e4m3":
        vals = words.view(ml_dtypes.float8_e4m3fn).astype(np.float64)
    else:
        nib = np.empty((g, 128, n, 4), np.uint8)
        nib[..., 0::2] = words & 0xF
        nib[..., 1::2] = words >> 4
        vals = E2M1[nib]
    vals = vals * np.repeat(np.exp2(scales.astype(np.float64) - 127.0), 8, axis=1)[..., None]
    return vals.transpose(0, 1, 3, 2).reshape(g * 512, n)


def sigmoid(v):
    return 1.0 / (1.0 + np.exp(-v))


D, T, I, Q = 512, 1024, 512, 128


def setup_inputs():
    n = np.random.standard_normal
    idx = np.stack([np.random.permutation(T)[:I] for _ in range(8)])
    idx2 = np.stack([np.random.permutation(T)[:I] for _ in range(8)])
    idx3 = np.stack([np.random.permutation(T)[:I] for _ in range(8)])
    idx4 = np.stack([np.random.permutation(T)[:I] for _ in range(8)])
    fd = mx_kscale(D)
    keysp = pack_weight(n((D, T)) / fd[:, None], "e4m3")
    return {
        "query": (n((D, Q)) * 0.9 / np.sqrt(D) * fd[:, None]).astype(np.float32),
        "keys_words": keysp[0],
        "keys_scales": keysp[1],
        "lam": (np.random.uniform(0.3, 0.9, (Q, 1))).astype(np.float32),
        "old": (np.random.uniform(0.3, 1.7, (Q, T))).astype(np.float32),
        "base": (0.5 * n((Q, T))).astype(np.float32),
        "offs": striped8(idx),
        "offs2": striped8(idx2),
        "offs3": striped8(idx3),
        "offs4": striped8(idx4),
    }


def reference(query, keys_words, keys_scales, lam, old, base, offs, offs2, offs3, offs4):
    idx = unstriped8(offs)
    idx2 = unstriped8(offs2)
    idx3 = unstriped8(offs3)
    idx4 = unstriped8(offs4)
    keysu = unpack_weight(keys_words, keys_scales, "e4m3")
    queryq = mxq(f64(query), 0, "e4m3")
    a = queryq.T @ keysu
    s = pick8(a, idx, 16) + np.maximum(pick8(a, idx2, 16), pick8(a, idx3, 16)) * f64(lam)
    w = sigmoid(s)
    ws = w * pick8(f64(old), idx4, 16)
    f1 = np.zeros((Q, T))
    f1[np.arange(Q)[:, None], idx[np.arange(Q) % 128 // 16]] = ws
    y = f64(base) + f1
    return y

@@ -1,0 +1,174 @@
+from contextlib import ExitStack
+
+import concourse.mybir as mybir
+
+D, T, I, Q = 512, 1024, 512, 128
+FLOPS = 2 * D * Q * T
+
+F32 = mybir.dt.float32
+BF16 = mybir.dt.bfloat16
+I32 = mybir.dt.int32
+U32 = mybir.dt.uint32
+U16 = mybir.dt.uint16
+U8 = mybir.dt.uint8
+FP8X4 = mybir.dt.float8_e4m3fn_x4
+ALU = mybir.AluOpType
+ACT = mybir.ActivationFunctionType
+
+P = 128
+PACK = 4
+STRIPE = 16
+HALF = I // 2
+QUARTER = I // 4
+KEY_CHUNK = T // 2
+MM_WIDTHS = (256, 256, 256, 256)
+OUT_WIDTHS = (128, 256, 256, 256, 128)
+
+
+def tile_attend_lookahead_lean_timesold_heads_kernel(
+    tc, query, keys_words, keys_scales, lam, old, base, offs, offs2, offs3, offs4, out
+):
+    nc = tc.nc
+    with ExitStack() as ctx:
+        pool = ctx.enter_context(tc.tile_pool(name="held", bufs=1))
+        psum = ctx.enter_context(tc.psum_pool(name="psum", bufs=1))
+
+        list1 = pool.tile([P, I // STRIPE], U16, name="list1")
+        list2 = pool.tile([P, I // STRIPE], U16, name="list2")
+        list3 = pool.tile([P, I // STRIPE], U16, name="list3")
+        list4 = pool.tile([P, I // STRIPE], U16, name="list4")
+        q_raw = pool.tile([P, PACK, Q], F32, name="q_raw")
+        q_bf = pool.tile([P, Q, PACK], BF16, name="q_bf", align_bytes=64)
+        q_codes = pool.tile([P, Q], U32, name="q_codes", align_bytes=64)
+        q_scales = pool.tile([P, Q], U8, name="q_scales", align_bytes=64)
+        k_codes = [pool.tile([P, KEY_CHUNK], U32, name="k_codes%d" % c, align_bytes=64) for c in range(2)]
+        k_scales = pool.tile([P, T], U8, name="k_scales", align_bytes=64)
+        scale_rows = pool.tile([P, 2, T], U8, name="scale_rows")
+        lam_sb = pool.tile([P, 1], F32, name="lam_sb")
+        old_sb = pool.tile([P, T], F32, name="old_sb")
+        base_sb = pool.tile([P, T], F32, name="base_sb")
+        a_sb = pool.tile([P, T], F32, name="a_sb")
+        placed = pool.tile([P, T], F32, name="placed")
+
+        nc.vector.memset(k_scales[:].bitcast(U32), 0)
+        nc.vector.memset(placed[:], 0.0)
+
+        for pair in range(2):
+            nc.scalar.dma_start(
+                scale_rows[64 * pair : 64 * pair + 4, :, :].bitcast(I32),
+                keys_scales[0, 8 * pair : 8 * pair + 8, :].rearrange("(e f) n -> f e n", e=2).bitcast(I32),
+            )
+        words = keys_words[0].rearrange("p n t -> p (n t)").bitcast(I32)
+        nc.sync.dma_start(q_raw[:], query.rearrange("(p j) q -> p j q", j=PACK))
+        for c in range(2):
+            nc.sync.dma_start(k_codes[c][:].bitcast(I32), words[:, c * KEY_CHUNK : (c + 1) * KEY_CHUNK])
+        nc.sync.dma_start(list4[:], offs4)
+        nc.sync.dma_start(old_sb[:], old)
+        nc.sync.dma_start(list3[:], offs3)
+        nc.sync.dma_start(list1[:], offs)
+        nc.sync.dma_start(list2[:], offs2)
+        nc.sync.dma_start(lam_sb[:], lam)
+        nc.sync.dma_start(base_sb[:], base)
+
+        def spread_scales(pair):
+            low = 64 * pair
+            nc.scalar.copy(
+                out=k_scales[low : low + 4, :].bitcast(U32), in_=scale_rows[low : low + 4, 0, :].bitcast(U32)
+            )
+            nc.vector.tensor_copy(
+                out=k_scales[low + 32 : low + 36, :].bitcast(I32), in_=scale_rows[low : low + 4, 1, :].bitcast(I32)
+            )
+
+        spread_scales(0)
+        nc.vector.tensor_copy(
+            out=q_bf[:].rearrange("p (c i) t -> p c t i", i=4),
+            in_=q_raw[:].rearrange("p t (c i) -> p c t i", i=4),
+        )
+        spread_scales(1)
+        nc.vector.quantize_mx(
+            out=q_codes[:].bitcast(FP8X4), scales=q_scales[:], in_=q_bf[:].rearrange("p q t -> p (q t)")
+        )
+
+        start = 0
+        for c, width in enumerate(MM_WIDTHS):
+            cols = slice(start, start + width)
+            within = slice(start % KEY_CHUNK, start % KEY_CHUNK + width)
+            acc = psum.tile([P, width], F32, name="acc%d" % c)
+            nc.tensor.matmul_mx(
+                out=acc[:],
+                lhsT=q_codes[:].bitcast(FP8X4),
+                lhsT_scale=q_scales[:],
+                rhs=k_codes[start // KEY_CHUNK][:, within].bitcast(FP8X4),
+                rhs_scale=k_scales[:, cols],
+                start=True,
+                stop=True,
+            )
+            nc.scalar.copy(out=a_sb[:, cols], in_=acc[:])
+            start = start + width
+
+        def entries(first, count):
+            return slice(first // STRIPE, (first + count) // STRIPE)
+
+        def half_tile(name):
+            return pool.tile([P, HALF], F32, name=name)
+
+        shared = pool.tile([P, 4, QUARTER], F32, name="shared")
+        flat = shared[:].rearrange("p a b -> p (a b)")
+        second = [half_tile("second0"), half_tile("second1")]
+        third = [half_tile("third0"), half_tile("third1")]
+        own = [flat[:, QUARTER : QUARTER + HALF], flat[:, 0:HALF]]
+        larger1 = flat[:, HALF : 2 * HALF]
+        score0 = half_tile("score0")
+        score1 = half_tile("score1")
+        weight = [half_tile("weight0"), half_tile("weight1")]
+        earlier = [half_tile("earlier0"), second[0]]
+
+        def scalar_gather(dst, window, lst, h):
+            nc.scalar.activation(dst, window[:].indirect(lst[:, entries(h * HALF, HALF)]), ACT.Copy)
+
+        def vector_gather(dst, window, lst, h):
+            nc.vector.tensor_copy(dst, window[:].indirect(lst[:, entries(h * HALF, HALF)]))
+
+        def make_score(dst, larger, own_part):
+            nc.vector.scalar_tensor_tensor(dst, larger, lam_sb[:], own_part, ALU.mult, ALU.add)
+
+        def place(h, first, count):
+            cols = slice(first, first + count)
+            nc.vector.tensor_tensor(
+                placed[:].indirect(list1[:, entries(h * HALF + first, count)]),
+                weight[h][:, cols],
+                earlier[h][:, cols],
+                ALU.mult,
+            )
+
+        lo = slice(0, QUARTER)
+        hi = slice(QUARTER, HALF)
+        vector_gather(earlier[0][:], old_sb, list4, 0)
+        scalar_gather(second[0][:], a_sb, list2, 0)
+        vector_gather(third[0][:], a_sb, list3, 0)
+        vector_gather(own[0], a_sb, list1, 0)
+        scalar_gather(second[1][:], a_sb, list2, 1)
+        scalar_gather(third[1][:], a_sb, list3, 1)
+        nc.vector.tensor_tensor(shared[:, 0, :], second[0][:, lo], third[0][:, lo], ALU.max)
+        nc.vector.tensor_tensor(shared[:, 3, :], second[0][:, hi], third[0][:, hi], ALU.max)
+        make_score(score0[:, lo], shared[:, 0, :], shared[:, 1, :])
+        make_score(score0[:, hi], shared[:, 3, :], shared[:, 2, :])
+        vector_gather(earlier[1][:], old_sb, list4, 1)
+        nc.scalar.activation(weight[0][:, lo], score0[:, lo], ACT.Sigmoid)
+        scalar_gather(own[1], a_sb, list1, 1)
+        nc.vector.tensor_tensor(larger1, second[1][:], third[1][:], ALU.max)
+        place(0, 0, QUARTER)
+        make_score(score1[:], larger1, own[1])
+        nc.scalar.activation(weight[0][:, hi], score0[:, hi], ACT.Sigmoid)
+        nc.scalar.activation(weight[1][:], score1[:], ACT.Sigmoid)
+        place(0, QUARTER, QUARTER)
+        place(1, 0, HALF)
+
+        start = 0
+        for c, width in enumerate(OUT_WIDTHS):
+            cols = slice(start, start + width)
+            result = pool.tile([P, width], F32, name="result%d" % c)
+            nc.vector.tensor_tensor(result[:], placed[:, cols], base_sb[:, cols], ALU.add)
+            queue = nc.sync if c % 2 == 0 else nc.scalar
+            queue.dma_start(out[:, cols], result[:])
+            start = start + width

@@ -70,6 +70,11 @@ def tile_attend_lookahead_lean_timesold_heads_kernel(
         nc.sync.dma_start(lam_sb[:], lam)
         nc.sync.dma_start(base_sb[:], base)
 
+        warm_in = pool.tile([P, 1], F32, name="warm_in")
+        warm_out = pool.tile([P, 1], F32, name="warm_out")
+        nc.gpsimd.memset(warm_in[:], 0.0)
+        nc.scalar.activation(warm_out[:], warm_in[:], ACT.Sigmoid)
+
         def spread_scales(pair):
             low = 64 * pair
             nc.scalar.copy(

@@ -20,8 +20,7 @@ PACK = 4
 STRIPE = 16
 HALF = I // 2
 QUARTER = I // 4
-KEY_CHUNK = T // 2
-MM_WIDTHS = (256, 256, 256, 256)
+MM_N = T // 4
 OUT_WIDTHS = (128, 256, 256, 256, 128)
 
 
@@ -41,9 +40,9 @@ def tile_attend_lookahead_lean_timesold_heads_kernel(
         q_bf = pool.tile([P, Q, PACK], BF16, name="q_bf", align_bytes=64)
         q_codes = pool.tile([P, Q], U32, name="q_codes", align_bytes=64)
         q_scales = pool.tile([P, Q], U8, name="q_scales", align_bytes=64)
-        k_codes = [pool.tile([P, KEY_CHUNK], U32, name="k_codes%d" % c, align_bytes=64) for c in range(2)]
-        k_scales = pool.tile([P, T], U8, name="k_scales", align_bytes=64)
-        scale_rows = pool.tile([P, 2, T], U8, name="scale_rows")
+        k_codes = pool.tile([P, T], U32, name="k_codes", align_bytes=64)
+        k_scales = pool.tile([P, MM_N], U8, name="k_scales", align_bytes=64)
+        scale_rows = pool.tile([P, MM_N], U8, name="scale_rows")
         lam_sb = pool.tile([P, 1], F32, name="lam_sb")
         old_sb = pool.tile([P, T], F32, name="old_sb")
         base_sb = pool.tile([P, T], F32, name="base_sb")
@@ -53,15 +52,14 @@ def tile_attend_lookahead_lean_timesold_heads_kernel(
         nc.vector.memset(k_scales[:].bitcast(U32), 0)
         nc.vector.memset(placed[:], 0.0)
 
-        for pair in range(2):
-            nc.scalar.dma_start(
-                scale_rows[64 * pair : 64 * pair + 4, :, :].bitcast(I32),
-                keys_scales[0, 8 * pair : 8 * pair + 8, :].rearrange("(e f) n -> f e n", e=2).bitcast(I32),
-            )
-        words = keys_words[0].rearrange("p n t -> p (n t)").bitcast(I32)
         nc.sync.dma_start(q_raw[:], query.rearrange("(p j) q -> p j q", j=PACK))
-        for c in range(2):
-            nc.sync.dma_start(k_codes[c][:].bitcast(I32), words[:, c * KEY_CHUNK : (c + 1) * KEY_CHUNK])
+        for quad in range(4):
+            queue = nc.scalar if quad < 2 else nc.sync
+            queue.dma_start(
+                scale_rows[32 * quad : 32 * quad + 16, :].bitcast(I32),
+                keys_scales[0, 4 * quad : 4 * quad + 4, :].rearrange("f (c n) -> c f n", c=4).bitcast(I32),
+            )
+        nc.sync.dma_start(k_codes[:].bitcast(I32), keys_words[0].rearrange("p n t -> p (n t)").bitcast(I32))
         nc.sync.dma_start(list4[:], offs4)
         nc.sync.dma_start(old_sb[:], old)
         nc.sync.dma_start(list3[:], offs3)
@@ -75,41 +73,31 @@ def tile_attend_lookahead_lean_timesold_heads_kernel(
         nc.gpsimd.memset(warm_in[:], 0.0)
         nc.scalar.activation(warm_out[:], warm_in[:], ACT.Sigmoid)
 
-        def spread_scales(pair):
-            low = 64 * pair
-            nc.scalar.copy(
-                out=k_scales[low : low + 4, :].bitcast(U32), in_=scale_rows[low : low + 4, 0, :].bitcast(U32)
-            )
-            nc.vector.tensor_copy(
-                out=k_scales[low + 32 : low + 36, :].bitcast(I32), in_=scale_rows[low : low + 4, 1, :].bitcast(I32)
-            )
+        for quad in range(4):
+            rows = slice(32 * quad, 32 * quad + 16)
+            nc.scalar.copy(out=k_scales[rows, :].bitcast(U32), in_=scale_rows[rows, :].bitcast(U32))
 
-        spread_scales(0)
         nc.vector.tensor_copy(
             out=q_bf[:].rearrange("p (c i) t -> p c t i", i=4),
             in_=q_raw[:].rearrange("p t (c i) -> p c t i", i=4),
         )
-        spread_scales(1)
         nc.vector.quantize_mx(
             out=q_codes[:].bitcast(FP8X4), scales=q_scales[:], in_=q_bf[:].rearrange("p q t -> p (q t)")
         )
 
-        start = 0
-        for c, width in enumerate(MM_WIDTHS):
-            cols = slice(start, start + width)
-            within = slice(start % KEY_CHUNK, start % KEY_CHUNK + width)
-            acc = psum.tile([P, width], F32, name="acc%d" % c)
+        for c in range(T // MM_N):
+            cols = slice(c * MM_N, (c + 1) * MM_N)
+            acc = psum.tile([P, MM_N], F32, name="acc%d" % c)
             nc.tensor.matmul_mx(
                 out=acc[:],
                 lhsT=q_codes[:].bitcast(FP8X4),
                 lhsT_scale=q_scales[:],
-                rhs=k_codes[start // KEY_CHUNK][:, within].bitcast(FP8X4),
-                rhs_scale=k_scales[:, cols],
+                rhs=k_codes[:, cols].bitcast(FP8X4),
+                rhs_scale=k_scales[4 * c : P, :],
                 start=True,
                 stop=True,
             )
             nc.scalar.copy(out=a_sb[:, cols], in_=acc[:])
-            start = start + width
 
         def entries(first, count):
             return slice(first // STRIPE, (first + count) // STRIPE)
@@ -126,7 +114,7 @@ def tile_attend_lookahead_lean_timesold_heads_kernel(
         score0 = half_tile("score0")
         score1 = half_tile("score1")
         weight = [half_tile("weight0"), half_tile("weight1")]
-        earlier = [half_tile("earlier0"), second[0]]
+        earlier = [half_tile("earlier0"), score0]
 
         def scalar_gather(dst, window, lst, h):
             nc.scalar.activation(dst, window[:].indirect(lst[:, entries(h * HALF, HALF)]), ACT.Copy)
@@ -158,13 +146,13 @@ def tile_attend_lookahead_lean_timesold_heads_kernel(
         nc.vector.tensor_tensor(shared[:, 3, :], second[0][:, hi], third[0][:, hi], ALU.max)
         make_score(score0[:, lo], shared[:, 0, :], shared[:, 1, :])
         make_score(score0[:, hi], shared[:, 3, :], shared[:, 2, :])
-        vector_gather(earlier[1][:], old_sb, list4, 1)
         nc.scalar.activation(weight[0][:, lo], score0[:, lo], ACT.Sigmoid)
         scalar_gather(own[1], a_sb, list1, 1)
         nc.vector.tensor_tensor(larger1, second[1][:], third[1][:], ALU.max)
         place(0, 0, QUARTER)
         make_score(score1[:], larger1, own[1])
         nc.scalar.activation(weight[0][:, hi], score0[:, hi], ACT.Sigmoid)
+        scalar_gather(earlier[1][:], old_sb, list4, 1)
         nc.scalar.activation(weight[1][:], score1[:], ACT.Sigmoid)
         place(0, QUARTER, QUARTER)
         place(1, 0, HALF)

from contextlib import ExitStack

import concourse.mybir as mybir

D, T, I, Q = 512, 1024, 512, 128
FLOPS = 2 * D * Q * T

F32 = mybir.dt.float32
BF16 = mybir.dt.bfloat16
I32 = mybir.dt.int32
U32 = mybir.dt.uint32
U16 = mybir.dt.uint16
U8 = mybir.dt.uint8
FP8X4 = mybir.dt.float8_e4m3fn_x4
ALU = mybir.AluOpType
ACT = mybir.ActivationFunctionType

P = 128
PACK = 4
STRIPE = 16
HALF = I // 2
QUARTER = I // 4
MM_N = T // 4
OUT_WIDTHS = (128, 256, 256, 256, 128)


def tile_attend_lookahead_lean_timesold_heads_kernel(
    tc, query, keys_words, keys_scales, lam, old, base, offs, offs2, offs3, offs4, out
):
    nc = tc.nc
    with ExitStack() as ctx:
        pool = ctx.enter_context(tc.tile_pool(name="held", bufs=1))
        psum = ctx.enter_context(tc.psum_pool(name="psum", bufs=1))

        list1 = pool.tile([P, I // STRIPE], U16, name="list1")
        list2 = pool.tile([P, I // STRIPE], U16, name="list2")
        list3 = pool.tile([P, I // STRIPE], U16, name="list3")
        list4 = pool.tile([P, I // STRIPE], U16, name="list4")
        q_raw = pool.tile([P, PACK, Q], F32, name="q_raw")
        q_bf = pool.tile([P, Q, PACK], BF16, name="q_bf", align_bytes=64)
        q_codes = pool.tile([P, Q], U32, name="q_codes", align_bytes=64)
        q_scales = pool.tile([P, Q], U8, name="q_scales", align_bytes=64)
        k_codes = pool.tile([P, T], U32, name="k_codes", align_bytes=64)
        k_scales = pool.tile([P, MM_N], U8, name="k_scales", align_bytes=64)
        scale_rows = pool.tile([P, MM_N], U8, name="scale_rows")
        lam_sb = pool.tile([P, 1], F32, name="lam_sb")
        old_sb = pool.tile([P, T], F32, name="old_sb")
        base_sb = pool.tile([P, T], F32, name="base_sb")
        a_sb = pool.tile([P, T], F32, name="a_sb")
        placed = pool.tile([P, T], F32, name="placed")

        nc.vector.memset(k_scales[:].bitcast(U32), 0)
        nc.vector.memset(placed[:], 0.0)

        nc.sync.dma_start(q_raw[:], query.rearrange("(p j) q -> p j q", j=PACK))
        for quad in range(4):
            queue = nc.scalar if quad < 2 else nc.sync
            queue.dma_start(
                scale_rows[32 * quad : 32 * quad + 16, :].bitcast(I32),
                keys_scales[0, 4 * quad : 4 * quad + 4, :].rearrange("f (c n) -> c f n", c=4).bitcast(I32),
            )
        nc.sync.dma_start(k_codes[:].bitcast(I32), keys_words[0].rearrange("p n t -> p (n t)").bitcast(I32))
        nc.sync.dma_start(list4[:], offs4)
        nc.sync.dma_start(old_sb[:], old)
        nc.sync.dma_start(list3[:], offs3)
        nc.sync.dma_start(list1[:], offs)
        nc.sync.dma_start(list2[:], offs2)
        nc.sync.dma_start(lam_sb[:], lam)
        nc.sync.dma_start(base_sb[:], base)

        warm_in = pool.tile([P, 1], F32, name="warm_in")
        warm_out = pool.tile([P, 1], F32, name="warm_out")
        nc.gpsimd.memset(warm_in[:], 0.0)
        nc.scalar.activation(warm_out[:], warm_in[:], ACT.Sigmoid)

        for quad in range(4):
            rows = slice(32 * quad, 32 * quad + 16)
            nc.scalar.copy(out=k_scales[rows, :].bitcast(U32), in_=scale_rows[rows, :].bitcast(U32))

        nc.vector.tensor_copy(
            out=q_bf[:].rearrange("p (c i) t -> p c t i", i=4),
            in_=q_raw[:].rearrange("p t (c i) -> p c t i", i=4),
        )
        nc.vector.quantize_mx(
            out=q_codes[:].bitcast(FP8X4), scales=q_scales[:], in_=q_bf[:].rearrange("p q t -> p (q t)")
        )

        for c in range(T // MM_N):
            cols = slice(c * MM_N, (c + 1) * MM_N)
            acc = psum.tile([P, MM_N], F32, name="acc%d" % c)
            nc.tensor.matmul_mx(
                out=acc[:],
                lhsT=q_codes[:].bitcast(FP8X4),
                lhsT_scale=q_scales[:],
                rhs=k_codes[:, cols].bitcast(FP8X4),
                rhs_scale=k_scales[4 * c : P, :],
                start=True,
                stop=True,
            )
            nc.scalar.copy(out=a_sb[:, cols], in_=acc[:])

        def entries(first, count):
            return slice(first // STRIPE, (first + count) // STRIPE)

        def half_tile(name):
            return pool.tile([P, HALF], F32, name=name)

        shared = pool.tile([P, 4, QUARTER], F32, name="shared")
        flat = shared[:].rearrange("p a b -> p (a b)")
        second = [half_tile("second0"), half_tile("second1")]
        third = [half_tile("third0"), half_tile("third1")]
        own = [flat[:, QUARTER : QUARTER + HALF], flat[:, 0:HALF]]
        larger1 = flat[:, HALF : 2 * HALF]
        score0 = half_tile("score0")
        score1 = half_tile("score1")
        weight = [half_tile("weight0"), half_tile("weight1")]
        earlier = [half_tile("earlier0"), score0]

        def scalar_gather(dst, window, lst, h):
            nc.scalar.activation(dst, window[:].indirect(lst[:, entries(h * HALF, HALF)]), ACT.Copy)

        def vector_gather(dst, window, lst, h):
            nc.vector.tensor_copy(dst, window[:].indirect(lst[:, entries(h * HALF, HALF)]))

        def make_score(dst, larger, own_part):
            nc.vector.scalar_tensor_tensor(dst, larger, lam_sb[:], own_part, ALU.mult, ALU.add)

        def place(h, first, count):
            cols = slice(first, first + count)
            nc.vector.tensor_tensor(
                placed[:].indirect(list1[:, entries(h * HALF + first, count)]),
                weight[h][:, cols],
                earlier[h][:, cols],
                ALU.mult,
            )

        lo = slice(0, QUARTER)
        hi = slice(QUARTER, HALF)
        vector_gather(earlier[0][:], old_sb, list4, 0)
        scalar_gather(second[0][:], a_sb, list2, 0)
        vector_gather(third[0][:], a_sb, list3, 0)
        vector_gather(own[0], a_sb, list1, 0)
        scalar_gather(second[1][:], a_sb, list2, 1)
        scalar_gather(third[1][:], a_sb, list3, 1)
        nc.vector.tensor_tensor(shared[:, 0, :], second[0][:, lo], third[0][:, lo], ALU.max)
        nc.vector.tensor_tensor(shared[:, 3, :], second[0][:, hi], third[0][:, hi], ALU.max)
        make_score(score0[:, lo], shared[:, 0, :], shared[:, 1, :])
        make_score(score0[:, hi], shared[:, 3, :], shared[:, 2, :])
        nc.scalar.activation(weight[0][:, lo], score0[:, lo], ACT.Sigmoid)
        scalar_gather(own[1], a_sb, list1, 1)
        nc.vector.tensor_tensor(larger1, second[1][:], third[1][:], ALU.max)
        place(0, 0, QUARTER)
        make_score(score1[:], larger1, own[1])
        nc.scalar.activation(weight[0][:, hi], score0[:, hi], ACT.Sigmoid)
        scalar_gather(earlier[1][:], old_sb, list4, 1)
        nc.scalar.activation(weight[1][:], score1[:], ACT.Sigmoid)
        place(0, QUARTER, QUARTER)
        place(1, 0, HALF)

        start = 0
        for c, width in enumerate(OUT_WIDTHS):
            cols = slice(start, start + width)
            result = pool.tile([P, width], F32, name="result%d" % c)
            nc.vector.tensor_tensor(result[:], placed[:, cols], base_sb[:, cols], ALU.add)
            queue = nc.sync if c % 2 == 0 else nc.scalar
            queue.dma_start(out[:, cols], result[:])
            start = start + width
